import numpy as np
import ml_dtypes


def mxq(x, axis, fmt="e4m3"):
    dtype, down = {"e4m3": (ml_dtypes.float8_e4m3fn, 7), "e5m2": (ml_dtypes.float8_e5m2, 14)}[fmt]
    v = np.moveaxis(np.asarray(x, np.float32).astype(ml_dtypes.bfloat16).astype(np.float64), axis, -1)
    blocks = v.reshape(v.shape[:-1] + (-1, 32))
    amax = np.abs(blocks).max(-1, keepdims=True)
    byte = np.maximum(np.where(amax > 0, np.frexp(amax)[1] - 1 + 127, 0) - down, 1)
    scale = np.exp2(byte - 127.0)
    codes = (blocks / scale).astype(np.float32).astype(dtype).astype(np.float64)
    return np.moveaxis((codes * scale).reshape(v.shape), -1, axis)


WIDE = False


def mx_kscale(k):
    if not WIDE:
        return np.ones(k)
    levels = np.array([10, -10, 5, -5, 0])
    if k % 512:
        return np.exp2(np.random.permutation(np.resize(levels, k // 32))).repeat(32)
    a = np.empty((k // 512, 16))
    for p in range(k // 512):
        a[p, :8] = np.random.permutation(np.resize(levels, 8))
        for g in range(8):
            far = levels[np.abs(levels - a[p, g]) >= 10]
            a[p, g + 8] = far[np.random.randint(len(far))]
    return np.exp2(a.ravel()).repeat(32)


def f64(x):
    return np.asarray(x).astype(np.float64)


def striped(idx):
    return np.tile(np.asarray(idx).reshape(-1, 16).T, (8, 1)).astype(np.uint16)


def unstriped(offs):
    return offs[:16].T.reshape(-1).astype(np.int64)


E2M1 = np.array([0.0, 0.5, 1.0, 1.5, 2.0, 3.0, 4.0, 6.0, -0.0, -0.5, -1.0, -1.5, -2.0, -3.0, -4.0, -6.0])


def pack_weight(w, fmt):
    k, n = w.shape
    w = f64(np.asarray(w, np.float32).astype(ml_dtypes.bfloat16)).reshape(k // 32, 32, n)
    amax = np.abs(w).max(1)
    if fmt == "e4m3":
        byte = np.frexp(amax)[1] - 1 + 127 - 7
    else:
        mant, ex = np.frexp(amax / 6.0)
        byte = np.where(mant > 0.5, ex, ex - 1) + 127
    byte = np.clip(np.where(amax > 0, byte, 1), 1, 254)
    scaled = (w * np.exp2(127.0 - byte)[:, None, :]).reshape(k, n).astype(np.float32)
    by_word = np.ascontiguousarray(scaled.reshape(k // 512, 128, 4, n).transpose(0, 1, 3, 2))
    if fmt == "e4m3":
        words = by_word.astype(ml_dtypes.float8_e4m3fn).view(np.uint8)
    else:
        c = by_word.astype(ml_dtypes.float4_e2m1fn).view(np.uint8) & 0xF
        words = (c[..., 0::2] | (c[..., 1::2] << 4)).reshape(k // 512, 128, 2 * n)
    return np.ascontiguousarray(words), np.ascontiguousarray(byte.astype(np.uint8).reshape(k // 512, 16, n))


def unpack_weight(words, scales, fmt):
    g, _, n = scales.shape
    words = np.ascontiguousarray(words).reshape(g, 128, n, -1)
    if fmt == "e4m3":
        vals = words.view(ml_dtypes.float8_e4m3fn).astype(np.float64)
    else:
        nib = np.empty((g, 128, n, 4), np.uint8)
        nib[..., 0::2] = words & 0xF
        nib[..., 1::2] = words >> 4
        vals = E2M1[nib]
    vals = vals * np.repeat(np.exp2(scales.astype(np.float64) - 127.0), 8, axis=1)[..., None]
    return vals.transpose(0, 1, 3, 2).reshape(g * 512, n)


def sigmoid(v):
    return 1.0 / (1.0 + np.exp(-v))


D, T, I, Q, E, U, M = 512, 2048, 512, 512, 512, 1024, 1024


def setup_inputs():
    n = np.random.standard_normal
    idx = np.random.permutation(T)[:I]
    idx2 = np.random.permutation(U)[:I]
    idx3 = np.random.permutation(M)[:I]
    fd = mx_kscale(D)
    fq = mx_kscale(Q)
    keysp = pack_weight(n((D, T)) / fd[:, None], "e2m1")
    return {
        "query": (n((D, Q)) * 0.9 / np.sqrt(D) * fd[:, None]).astype(np.float32),
        "keys_words": keysp[0],
        "keys_scales": keysp[1],
        "query2": (n((D, Q)) * 0.9 / np.sqrt(D) * fd[:, None]).astype(np.float32),
        "notes": (n((D, U)) / fd[:, None]).astype(np.float32),
        "lam": (np.random.uniform(0.1, 0.5, (Q, 1))).astype(np.float32),
        "qs": (np.random.uniform(0.5, 2.0, (Q, 1)) * fq[:, None]).astype(np.float32),
        "msgs": (n((Q, E)) * 1 / np.sqrt(Q) / fq[:, None]).astype(np.float32),
        "old": (n((E, M)) * 1.0).astype(np.float32),
        "fade": (np.random.uniform(0.3, 0.9, (1, M))).astype(np.float32),
        "offs": striped(idx),
        "offs2": striped(idx2),
        "offs3": striped(idx3),
    }


def reference(query, keys_words, keys_scales, query2, notes, lam, qs, msgs, old, fade, offs, offs2, offs3):
    idx = unstriped(offs)
    idx2 = unstriped(offs2)
    idx3 = unstriped(offs3)
    keysu = unpack_weight(keys_words, keys_scales, "e2m1")
    queryq = mxq(f64(query), 0, "e4m3")
    keysidxg = keysu[:, idx]
    a = queryq.T @ keysidxg
    query2q = mxq(f64(query2), 0, "e4m3")
    notesidx2q = mxq(f64(notes)[:, idx2], 0, "e4m3")
    b = query2q.T @ notesidx2q
    s = np.maximum(a, b) + np.minimum(a, b) * f64(lam)
    w = sigmoid(s)
    wq = w * f64(qs)
    msgsq = mxq(f64(msgs), 0, "e4m3")
    wqq = mxq(wq, 0, "e4m3")
    dl = msgsq.T @ wqq
    df = np.zeros((E, M))
    df[:, idx3] = dl
    y = f64(old) * f64(fade) + df
    return y

@@ -1,0 +1,236 @@
+from contextlib import ExitStack
+
+import concourse.mybir as mybir
+
+D, T, I, Q, E, U, M = 512, 2048, 512, 512, 512, 1024, 1024
+FLOPS = 3 * 2 * 512 * 512 * 512
+
+F32 = mybir.dt.float32
+BF16 = mybir.dt.bfloat16
+I32 = mybir.dt.int32
+U32 = mybir.dt.uint32
+U16 = mybir.dt.uint16
+U8 = mybir.dt.uint8
+FP8X4 = mybir.dt.float8_e4m3fn_x4
+FP4X4 = mybir.dt.float4_e2m1fn_x4
+ALU = mybir.AluOpType
+ACT = mybir.ActivationFunctionType
+
+P = 128
+PACK = 4
+PIECE = 128
+PIECES = I // PIECE
+OFFS_COLS = PIECE // 16
+
+
+def tile_attend_twopools_delivered_lean_kernel(
+    tc, query, keys_words, keys_scales, query2, notes, lam, qs, msgs, old, fade, offs, offs2, offs3, out
+):
+    nc = tc.nc
+    with ExitStack() as ctx:
+        sb = ctx.enter_context(tc.tile_pool(name="sb", bufs=1))
+        ps = ctx.enter_context(tc.psum_pool(name="ps", bufs=1))
+
+        def tile(name, shape, dtype):
+            return sb.tile(shape, dtype, name=name, align_bytes=64)
+
+        def quantise(codes, scales, grouped):
+            nc.vector.quantize_mx(out=codes.bitcast(FP8X4), scales=scales, in_=grouped)
+
+        key_list = tile("key_list", [P, I // 16], U16)
+        note_list = tile("note_list", [P, I // 16], U16)
+        place_list = tile("place_list", [P, I // 16], U16)
+        key_words = tile("key_words", [P, T], U16)
+        key_bytes = tile("key_bytes", [P, T], U8)
+        q_raw = tile("q_raw", [P, PACK, Q], F32)
+        q2_halves = [tile("q2_raw%d" % h, [P, PACK, Q // 2], F32) for h in range(2)]
+        msgs_raw = tile("msgs_raw", [P, PACK, E], F32)
+        note_planes = [tile("note_plane%d" % j, [P, U], F32) for j in range(PACK)]
+        old_tiles = [tile("old%d" % t, [P, M], F32) for t in range(E // P)]
+        fade_rows = tile("fade_rows", [P, M], F32)
+        lam_cols = tile("lam_cols", [P, PACK], F32)
+        qs_cols = tile("qs_cols", [P, PACK], F32)
+        windows = [tile("window%d" % t, [P, M], F32) for t in range(E // P)]
+
+        nc.vector.memset(key_bytes[:].bitcast(I32), 0)
+        nc.sync.dma_start(key_words[:].bitcast(I32), keys_words[0].bitcast(I32))
+        nc.sync.dma_start(key_list[:], offs)
+        for quad in range(4):
+            nc.sync.dma_start(
+                key_bytes[32 * quad : 32 * quad + 4, :].bitcast(I32),
+                keys_scales[0, 4 * quad : 4 * quad + 4, :].bitcast(I32),
+            )
+        nc.gpsimd.dma_start(lam_cols[:], lam.rearrange("(p r) o -> p (r o)", r=PACK))
+        nc.gpsimd.dma_start(qs_cols[:], qs.rearrange("(p r) o -> p (r o)", r=PACK))
+        nc.sync.dma_start(q_raw[:], query.rearrange("(p j) c -> p j c", j=PACK))
+        notes_by_plane = notes.rearrange("(p j) u -> p j u", j=PACK)
+        nc.sync.dma_start(note_planes[0][:], notes_by_plane[:, 0, :])
+        nc.sync.dma_start(note_list[:], offs2)
+        for j in range(1, PACK):
+            nc.sync.dma_start(note_planes[j][:], notes_by_plane[:, j, :])
+        for h in range(2):
+            nc.sync.dma_start(
+                q2_halves[h][:], query2.rearrange("(p j) c -> p j c", j=PACK)[:, :, h * (Q // 2) : (h + 1) * (Q // 2)]
+            )
+        nc.sync.dma_start(msgs_raw[:], msgs.rearrange("(p j) c -> p j c", j=PACK))
+        nc.sync.dma_start(place_list[:], offs3)
+        nc.sync.dma_start(fade_rows[:], fade[0].partition_broadcast(P))
+        for t in range(E // P):
+            nc.sync.dma_start(old_tiles[t][:], old[t * P : (t + 1) * P, :])
+
+        for t in range(E // P):
+            nc.gpsimd.memset(windows[t][:], 0.0)
+
+        kg_words = tile("kg_words", [P, I], U16)
+        kg_bytes = tile("kg_bytes", [P, I], U8)
+        nc.vector.tensor_copy(kg_words[:], key_words[:].indirect(key_list[:]))
+
+        q_grouped = tile("q_grouped", [P, Q * PACK], BF16)
+        q_codes = tile("q_codes", [P, Q], U32)
+        q_scales = tile("q_scales", [P, Q], U8)
+        nc.vector.tensor_copy(
+            q_grouped[:].rearrange("p (r m j) -> p m j r", r=PACK, j=PACK),
+            q_raw[:].rearrange("p j (m r) -> p m j r", r=PACK),
+        )
+        quantise(q_codes[:], q_scales[:], q_grouped[:])
+        nc.vector.tensor_copy(kg_bytes[:], key_bytes[:].indirect(key_list[:]))
+
+        lam_less_one = tile("lam_less_one", [P, PACK], F32)
+        nc.vector.tensor_scalar(lam_less_one[:], lam_cols[:], -1.0, None, ALU.add)
+
+        a_banks = [ps.tile([P, PACK, PIECE], F32, name="a_bank%d" % n) for n in range(PIECES)]
+        a_sb = [tile("a_sb%d" % n, [P, PACK, PIECE], F32) for n in range(PIECES)]
+        for n in range(PIECES):
+            cols = slice(n * PIECE, (n + 1) * PIECE)
+            for r in range(PACK):
+                rows = slice(r * P, (r + 1) * P)
+                nc.tensor.matmul_mx(
+                    out=a_banks[n][:, r, :],
+                    lhsT=q_codes[:, rows].bitcast(FP8X4), lhsT_scale=q_scales[:, rows],
+                    rhs=kg_words[:, cols].bitcast(FP4X4), rhs_scale=kg_bytes[:, cols],
+                    start=True, stop=True,
+                )
+            nc.scalar.copy(a_sb[n][:], a_banks[n][:])
+
+        ng_all = tile("ng_all", [P, PACK, I], BF16)
+        nc.scalar.activation(ng_all[:, 0, :], note_planes[0][:].indirect(note_list[:]), ACT.Copy)
+        for j in range(1, PACK):
+            nc.vector.tensor_copy(ng_all[:, j, :], note_planes[j][:].indirect(note_list[:]))
+
+        q2_grouped = tile("q2_grouped", [P, Q * PACK], BF16)
+        q2_codes = tile("q2_codes", [P, Q], U32)
+        q2_scales = tile("q2_scales", [P, Q], U8)
+        q2_view = q2_grouped[:].rearrange("p (r m j) -> p m j r", r=PACK, j=PACK)
+        nc.scalar.copy(q2_view[:, 0 : P // 2], q2_halves[0][:].rearrange("p j (m r) -> p m j r", r=PACK))
+
+        n_codes = tile("n_codes", [P, I], U32)
+        n_scales = tile("n_scales", [P, I], U8)
+
+        def quantise_notes(n):
+            cols = slice(n * PIECE, (n + 1) * PIECE)
+            grouped = tile("n_grouped%d" % n, [P, PIECE * PACK], BF16)
+            dst = grouped[:].rearrange("p (c i j) -> p c j i", i=4, j=PACK)
+            src = ng_all[:, :, cols].rearrange("p j (c i) -> p c j i", i=4)
+            if n == 0:
+                nc.vector.tensor_copy(dst, src)
+            else:
+                nc.scalar.copy(dst, src)
+            quantise(n_codes[:, cols], n_scales[:, cols], grouped[:])
+
+        m_grouped = tile("m_grouped", [P, E * PACK], BF16)
+        m_codes = tile("m_codes", [P, E], U32)
+        m_scales = tile("m_scales", [P, E], U8)
+
+        def scores(n):
+            cols = slice(n * PIECE, (n + 1) * PIECE)
+            b_bank = ps.tile([P, PACK, PIECE], F32, name="b_bank", bufs=2)
+            for r in range(PACK):
+                rows = slice(r * P, (r + 1) * P)
+                nc.tensor.matmul_mx(
+                    out=b_bank[:, r, :],
+                    lhsT=q2_codes[:, rows].bitcast(FP8X4), lhsT_scale=q2_scales[:, rows],
+                    rhs=n_codes[:, cols].bitcast(FP8X4), rhs_scale=n_scales[:, cols],
+                    start=True, stop=True,
+                )
+            smaller = tile("smaller%d" % n, [P, PACK, PIECE], F32)
+            part = tile("part%d" % n, [P, PACK, PIECE], F32)
+            s = tile("s%d" % n, [P, PIECE * PACK], F32)
+            w = tile("w%d" % n, [P, PIECE, PACK], F32)
+            nc.vector.tensor_tensor(smaller[:], b_bank[:], a_sb[n][:], ALU.min)
+            for r in range(PACK):
+                nc.vector.scalar_tensor_tensor(
+                    part[:, r, :], smaller[:, r, :], lam_less_one[:, r : r + 1], b_bank[:, r, :], ALU.mult, ALU.add
+                )
+            nc.vector.tensor_tensor(
+                s[:].rearrange("p (c i r) -> p c r i", i=4, r=PACK),
+                part[:].rearrange("p r (c i) -> p c r i", i=4),
+                a_banks[n][:].rearrange("p r (c i) -> p c r i", i=4),
+                ALU.add,
+            )
+            nc.scalar.activation(w[:].rearrange("p i r -> p (i r)"), s[:], ACT.Sigmoid)
+            return w
+
+        def deliver(n, w):
+            wq = tile("wq%d" % n, [P, PIECE, PACK], BF16)
+            wq_codes = tile("wq_codes%d" % n, [P, PIECE], U32)
+            wq_scales = tile("wq_scales%d" % n, [P, PIECE], U8)
+            nc.vector.tensor_tensor(wq[:], w[:], qs_cols[:].unsqueeze(1).to_broadcast([P, PIECE, PACK]), ALU.mult)
+            quantise(wq_codes[:], wq_scales[:], wq[:].rearrange("p i r -> p (i r)"))
+            pair_bank = ps.tile([P, PACK, PIECE], F32, name="a_bank%d" % n)
+            for t in range(E // P):
+                rows = slice(t * P, (t + 1) * P)
+                nc.tensor.matmul_mx(
+                    out=pair_bank[:, t, :] if t < 2 else late_banks[t - 2][:, n * PIECE : (n + 1) * PIECE],
+                    lhsT=m_codes[:, rows].bitcast(FP8X4), lhsT_scale=m_scales[:, rows],
+                    rhs=wq_codes[:].bitcast(FP8X4), rhs_scale=wq_scales[:],
+                    start=True, stop=True,
+                )
+            dl = tile("dl%d" % n, [P, 2, PIECE], F32)
+            nc.scalar.copy(dl[:], pair_bank[:, 0:2, :])
+            places = place_list[:, n * OFFS_COLS : (n + 1) * OFFS_COLS]
+            for t in range(2):
+                nc.scalar.activation(windows[t][:].indirect(places), dl[:, t, :], ACT.Copy)
+
+        late_banks = [ps.tile([P, I], F32, name="late_bank%d" % t) for t in range(2)]
+        quantise_notes(0)
+        nc.vector.tensor_copy(q2_view[:, P // 2 : P], q2_halves[1][:].rearrange("p j (m r) -> p m j r", r=PACK))
+        quantise(q2_codes[:], q2_scales[:], q2_grouped[:])
+        for h in range(2):
+            cols = slice(h * (E // 2), (h + 1) * (E // 2))
+            nc.gpsimd.tensor_scalar(
+                m_grouped[:, h * 2 * E : (h + 1) * 2 * E].rearrange("p (c i j) -> p c j i", i=4, j=PACK),
+                msgs_raw[:, :, cols].rearrange("p j (c i) -> p c j i", i=4),
+                1.0, 0.0, ALU.mult, ALU.add,
+            )
+        faded = [tile("faded%d" % t, [P, M], F32) for t in range(E // P)]
+        for n in range(PIECES):
+            w = scores(n)
+            if n == 0:
+                for h in range(2):
+                    cols = slice(h * (E // 2), (h + 1) * (E // 2))
+                    quantise(m_codes[:, cols], m_scales[:, cols], m_grouped[:, h * 2 * E : (h + 1) * 2 * E])
+            deliver(n, w)
+            if n + 1 < PIECES:
+                quantise_notes(n + 1)
+
+        late3 = tile("late3", [P, I], F32)
+        nc.vector.tensor_copy(late3[:], late_banks[1][:])
+        nc.vector.tensor_copy(windows[3][:].indirect(place_list[:]), late3[:])
+        late2 = tile("late2", [P, I], F32)
+        nc.scalar.copy(late2[:], late_banks[0][:])
+        for h in range(2):
+            nc.scalar.activation(
+                windows[2][:].indirect(place_list[:, 16 * h : 16 * h + 16]), late2[:, 256 * h : 256 * h + 256], ACT.Copy
+            )
+
+        for t in (0, 1, 3, 2):
+            for c in range(4):
+                cols = slice(c * (M // 4), (c + 1) * (M // 4))
+                nc.gpsimd.tensor_tensor(faded[t][:, cols], old_tiles[t][:, cols], fade_rows[:, cols], ALU.mult)
+        for t in (0, 1, 3, 2):
+            res = tile("res%d" % t, [P, M], F32)
+            cuts = 2 if t == 2 else 1
+            for c in range(cuts):
+                cols = slice(c * (M // cuts), (c + 1) * (M // cuts))
+                nc.vector.tensor_tensor(res[:, cols], faded[t][:, cols], windows[t][:, cols], ALU.add)
+                nc.sync.dma_start(out[t * P : (t + 1) * P, cols], res[:, cols])

@@ -1,6 +1,7 @@
 from contextlib import ExitStack
 
 import concourse.mybir as mybir
+from concourse.masks import make_identity
 
 D, T, I, Q, E, U, M = 512, 2048, 512, 512, 512, 1024, 1024
 FLOPS = 3 * 2 * 512 * 512 * 512
@@ -21,6 +22,9 @@ PACK = 4
 PIECE = 128
 PIECES = I // PIECE
 OFFS_COLS = PIECE // 16
+TILES = E // P
+FADE_COLS = M // P
+FADE_CUTS = 4
 
 
 def tile_attend_twopools_delivered_lean_kernel(
@@ -29,6 +33,7 @@ def tile_attend_twopools_delivered_lean_kernel(
     nc = tc.nc
     with ExitStack() as ctx:
         sb = ctx.enter_context(tc.tile_pool(name="sb", bufs=1))
+        shared = ctx.enter_context(tc.tile_pool(name="shared", bufs=1))
         ps = ctx.enter_context(tc.psum_pool(name="ps", bufs=1))
 
         def tile(name, shape, dtype):
@@ -37,34 +42,46 @@ def tile_attend_twopools_delivered_lean_kernel(
         def quantise(codes, scales, grouped):
             nc.vector.quantize_mx(out=codes.bitcast(FP8X4), scales=scales, in_=grouped)
 
+        def product(dst, stat_codes, stat_scales, mov_codes, mov_scales):
+            nc.tensor.matmul_mx(
+                out=dst, lhsT=stat_codes, lhsT_scale=stat_scales, rhs=mov_codes, rhs_scale=mov_scales,
+                start=True, stop=True,
+            )
+
         key_list = tile("key_list", [P, I // 16], U16)
         note_list = tile("note_list", [P, I // 16], U16)
         place_list = tile("place_list", [P, I // 16], U16)
         key_words = tile("key_words", [P, T], U16)
         key_bytes = tile("key_bytes", [P, T], U8)
         q_raw = tile("q_raw", [P, PACK, Q], F32)
-        q2_halves = [tile("q2_raw%d" % h, [P, PACK, Q // 2], F32) for h in range(2)]
+        q2_halves = [shared.tile([P, PACK, Q // 2], F32, name="q2_raw%d" % h, offset=4096 * h, align_bytes=64) for h in range(2)]
         msgs_raw = tile("msgs_raw", [P, PACK, E], F32)
         note_planes = [tile("note_plane%d" % j, [P, U], F32) for j in range(PACK)]
-        old_tiles = [tile("old%d" % t, [P, M], F32) for t in range(E // P)]
-        fade_rows = tile("fade_rows", [P, M], F32)
+        old_tiles = [tile("old%d" % t, [P, M], F32) for t in range(TILES)]
+        fade_cols = tile("fade_cols", [P, FADE_COLS], F32)
         lam_cols = tile("lam_cols", [P, PACK], F32)
         qs_cols = tile("qs_cols", [P, PACK], F32)
-        windows = [tile("window%d" % t, [P, M], F32) for t in range(E // P)]
+        windows = [tile("window%d" % t, [P, M], F32) for t in range(TILES)]
+        ident = tile("ident", [P, P], F32)
+
+        make_identity(nc, ident[:])
+        nc.gpsimd.dma_start(lam_cols[:], lam.rearrange("(p r) o -> p (r o)", r=PACK))
+        nc.sync.dma_start(qs_cols[:], qs.rearrange("(p r) o -> p (r o)", r=PACK))
+        nc.sync.dma_start(fade_cols[:], fade.rearrange("o (p c) -> p (o c)", c=FADE_COLS))
+        warm = tile("warm", [P, 1], F32)
+        nc.scalar.activation(warm[:], ident[:, 0:1], ACT.Sigmoid)
 
         nc.vector.memset(key_bytes[:].bitcast(I32), 0)
         nc.sync.dma_start(key_words[:].bitcast(I32), keys_words[0].bitcast(I32))
         nc.sync.dma_start(key_list[:], offs)
+        nc.sync.dma_start(q_raw[:], query.rearrange("(p j) c -> p j c", j=PACK))
+        notes_by_plane = notes.rearrange("(p j) u -> p j u", j=PACK)
+        nc.sync.dma_start(note_planes[0][:], notes_by_plane[:, 0, :])
         for quad in range(4):
             nc.sync.dma_start(
                 key_bytes[32 * quad : 32 * quad + 4, :].bitcast(I32),
                 keys_scales[0, 4 * quad : 4 * quad + 4, :].bitcast(I32),
             )
-        nc.gpsimd.dma_start(lam_cols[:], lam.rearrange("(p r) o -> p (r o)", r=PACK))
-        nc.gpsimd.dma_start(qs_cols[:], qs.rearrange("(p r) o -> p (r o)", r=PACK))
-        nc.sync.dma_start(q_raw[:], query.rearrange("(p j) c -> p j c", j=PACK))
-        notes_by_plane = notes.rearrange("(p j) u -> p j u", j=PACK)
-        nc.sync.dma_start(note_planes[0][:], notes_by_plane[:, 0, :])
         nc.sync.dma_start(note_list[:], offs2)
         for j in range(1, PACK):
             nc.sync.dma_start(note_planes[j][:], notes_by_plane[:, j, :])
@@ -74,48 +91,54 @@ def tile_attend_twopools_delivered_lean_kernel(
             )
         nc.sync.dma_start(msgs_raw[:], msgs.rearrange("(p j) c -> p j c", j=PACK))
         nc.sync.dma_start(place_list[:], offs3)
-        nc.sync.dma_start(fade_rows[:], fade[0].partition_broadcast(P))
-        for t in range(E // P):
+        order = [TILES - 1] + list(range(TILES - 1))
+        for t in order:
             nc.sync.dma_start(old_tiles[t][:], old[t * P : (t + 1) * P, :])
 
-        for t in range(E // P):
-            nc.gpsimd.memset(windows[t][:], 0.0)
+        for t in range(TILES):
+            nc.vector.memset(windows[t][:], 0.0) if t < 2 else nc.gpsimd.memset(windows[t][:], 0.0)
+
+        qs_rows_bank = ps.tile([P, PACK, P], F32, name="b_bank", bufs=2)
+        for r in range(PACK):
+            nc.tensor.transpose(qs_rows_bank[:, r, :], qs_cols[:, r : r + 1].to_broadcast([P, P]), ident[:])
+        qs_rows = tile("qs_rows", [P, PACK, P], F32)
+        nc.scalar.copy(qs_rows[:], qs_rows_bank[:])
+        qs_bank = ps.tile([P, PACK, PIECE], F32, name="qs_bank")
+        for r in range(PACK):
+            nc.tensor.transpose(qs_bank[:, r, :], qs_rows[:, r, :], ident[:])
+        fade_rows = tile("fade_rows", [P, M], F32)
+        for h in range(2):
+            fade_bank = ps.tile([P, 4, P], F32, name="b_bank", bufs=2)
+            for c in range(4):
+                col = 4 * h + c
+                nc.tensor.transpose(fade_bank[:, c, :], fade_cols[:, col : col + 1].to_broadcast([P, P]), ident[:])
+            nc.scalar.copy(
+                fade_rows[:].rearrange("p (n c) -> p n c", c=FADE_COLS)[:, :, 4 * h : 4 * h + 4],
+                fade_bank[:].rearrange("p c n -> p n c"),
+            )
 
         kg_words = tile("kg_words", [P, I], U16)
         kg_bytes = tile("kg_bytes", [P, I], U8)
         nc.vector.tensor_copy(kg_words[:], key_words[:].indirect(key_list[:]))
-
         q_grouped = tile("q_grouped", [P, Q * PACK], BF16)
         q_codes = tile("q_codes", [P, Q], U32)
         q_scales = tile("q_scales", [P, Q], U8)
-        nc.vector.tensor_copy(
-            q_grouped[:].rearrange("p (r m j) -> p m j r", r=PACK, j=PACK),
-            q_raw[:].rearrange("p j (m r) -> p m j r", r=PACK),
+        nc.gpsimd.tensor_scalar(
+            q_grouped[:].rearrange("p (r m j) -> p r m j", r=PACK, j=PACK),
+            q_raw[:].rearrange("p j (m r) -> p r m j", r=PACK),
+            1.0, 0.0, ALU.mult, ALU.add,
         )
-        quantise(q_codes[:], q_scales[:], q_grouped[:])
         nc.vector.tensor_copy(kg_bytes[:], key_bytes[:].indirect(key_list[:]))
-
+        quantise(q_codes[:], q_scales[:], q_grouped[:])
         lam_less_one = tile("lam_less_one", [P, PACK], F32)
-        nc.vector.tensor_scalar(lam_less_one[:], lam_cols[:], -1.0, None, ALU.add)
-
-        a_banks = [ps.tile([P, PACK, PIECE], F32, name="a_bank%d" % n) for n in range(PIECES)]
-        a_sb = [tile("a_sb%d" % n, [P, PACK, PIECE], F32) for n in range(PIECES)]
-        for n in range(PIECES):
-            cols = slice(n * PIECE, (n + 1) * PIECE)
-            for r in range(PACK):
-                rows = slice(r * P, (r + 1) * P)
-                nc.tensor.matmul_mx(
-                    out=a_banks[n][:, r, :],
-                    lhsT=q_codes[:, rows].bitcast(FP8X4), lhsT_scale=q_scales[:, rows],
-                    rhs=kg_words[:, cols].bitcast(FP4X4), rhs_scale=kg_bytes[:, cols],
-                    start=True, stop=True,
-                )
-            nc.scalar.copy(a_sb[n][:], a_banks[n][:])
+        nc.gpsimd.tensor_scalar(lam_less_one[:], lam_cols[:], 1.0, -1.0, ALU.mult, ALU.add)
 
         ng_all = tile("ng_all", [P, PACK, I], BF16)
-        nc.scalar.activation(ng_all[:, 0, :], note_planes[0][:].indirect(note_list[:]), ACT.Copy)
-        for j in range(1, PACK):
-            nc.vector.tensor_copy(ng_all[:, j, :], note_planes[j][:].indirect(note_list[:]))
+        for j in range(PACK):
+            if j == 2:
+                nc.scalar.activation(ng_all[:, j, :], note_planes[j][:].indirect(note_list[:]), ACT.Copy)
+            else:
+                nc.vector.tensor_copy(ng_all[:, j, :], note_planes[j][:].indirect(note_list[:]))
 
         q2_grouped = tile("q2_grouped", [P, Q * PACK], BF16)
         q2_codes = tile("q2_codes", [P, Q], U32)
@@ -126,110 +149,167 @@ def tile_attend_twopools_delivered_lean_kernel(
         n_codes = tile("n_codes", [P, I], U32)
         n_scales = tile("n_scales", [P, I], U8)
 
-        def quantise_notes(n):
+        n_grouped = [
+            shared.tile([P, PIECE * PACK], BF16, name="n_grouped%d" % n, offset=off, align_bytes=64)
+            for n, off in enumerate((10240, 2048, 3072, 11264))
+        ]
+
+        def group_notes(n):
             cols = slice(n * PIECE, (n + 1) * PIECE)
-            grouped = tile("n_grouped%d" % n, [P, PIECE * PACK], BF16)
+            grouped = n_grouped[n]
             dst = grouped[:].rearrange("p (c i j) -> p c j i", i=4, j=PACK)
             src = ng_all[:, :, cols].rearrange("p j (c i) -> p c j i", i=4)
             if n == 0:
                 nc.vector.tensor_copy(dst, src)
             else:
                 nc.scalar.copy(dst, src)
-            quantise(n_codes[:, cols], n_scales[:, cols], grouped[:])
+
+        def quantise_notes(n):
+            cols = slice(n * PIECE, (n + 1) * PIECE)
+            quantise(n_codes[:, cols], n_scales[:, cols], n_grouped[n][:])
 
         m_grouped = tile("m_grouped", [P, E * PACK], BF16)
         m_codes = tile("m_codes", [P, E], U32)
         m_scales = tile("m_scales", [P, E], U8)
 
-        def scores(n):
+        b_banks, smaller, part, w_tiles, wq_tiles, dl_banks = {}, {}, {}, {}, {}, {}
+        late_bank = ps.tile([P, I], F32, name="late_bank")
+
+        def take_smaller(n):
             cols = slice(n * PIECE, (n + 1) * PIECE)
-            b_bank = ps.tile([P, PACK, PIECE], F32, name="b_bank", bufs=2)
+            b_banks[n] = ps.tile([P, PACK, PIECE], F32, name="b_bank", bufs=2)
             for r in range(PACK):
                 rows = slice(r * P, (r + 1) * P)
-                nc.tensor.matmul_mx(
-                    out=b_bank[:, r, :],
-                    lhsT=q2_codes[:, rows].bitcast(FP8X4), lhsT_scale=q2_scales[:, rows],
-                    rhs=n_codes[:, cols].bitcast(FP8X4), rhs_scale=n_scales[:, cols],
-                    start=True, stop=True,
-                )
-            smaller = tile("smaller%d" % n, [P, PACK, PIECE], F32)
-            part = tile("part%d" % n, [P, PACK, PIECE], F32)
-            s = tile("s%d" % n, [P, PIECE * PACK], F32)
-            w = tile("w%d" % n, [P, PIECE, PACK], F32)
-            nc.vector.tensor_tensor(smaller[:], b_bank[:], a_sb[n][:], ALU.min)
+                product(b_banks[n][:, r, :], q2_codes[:, rows].bitcast(FP8X4), q2_scales[:, rows],
+                        n_codes[:, cols].bitcast(FP8X4), n_scales[:, cols])
+            smaller[n] = tile("smaller%d" % n, [P, PACK, PIECE], F32)
+            nc.vector.tensor_tensor(smaller[n][:], b_banks[n][:], a_sb[n][:], ALU.min)
+
+        def add_b(n):
+            part[n] = tile("part%d" % n, [P, PACK, PIECE], F32)
             for r in range(PACK):
                 nc.vector.scalar_tensor_tensor(
-                    part[:, r, :], smaller[:, r, :], lam_less_one[:, r : r + 1], b_bank[:, r, :], ALU.mult, ALU.add
+                    part[n][:, r, :], smaller[n][:, r, :], lam_less_one[:, r : r + 1], b_banks[n][:, r, :],
+                    ALU.mult, ALU.add,
                 )
+
+        def add_a(n):
+            s = tile("s_then_dl%d" % n, [P, PIECE * PACK], F32)
+            w_tiles[n] = tile("w%d" % n, [P, PIECE * PACK], F32)
             nc.vector.tensor_tensor(
                 s[:].rearrange("p (c i r) -> p c r i", i=4, r=PACK),
-                part[:].rearrange("p r (c i) -> p c r i", i=4),
+                part[n][:].rearrange("p r (c i) -> p c r i", i=4),
                 a_banks[n][:].rearrange("p r (c i) -> p c r i", i=4),
                 ALU.add,
             )
-            nc.scalar.activation(w[:].rearrange("p i r -> p (i r)"), s[:], ACT.Sigmoid)
-            return w
+            nc.scalar.activation(w_tiles[n][:], s[:], ACT.Sigmoid)
 
-        def deliver(n, w):
-            wq = tile("wq%d" % n, [P, PIECE, PACK], BF16)
+        def weigh(n):
+            wq_tiles[n] = tile("wq%d" % n, [P, PIECE * PACK], BF16)
+            nc.vector.tensor_tensor(
+                wq_tiles[n][:].rearrange("p (i r) -> p i r", r=PACK),
+                w_tiles[n][:].rearrange("p (i r) -> p i r", r=PACK),
+                qs_bank[:].rearrange("p r i -> p i r"),
+                ALU.mult,
+            )
+
+        def messages(n):
             wq_codes = tile("wq_codes%d" % n, [P, PIECE], U32)
             wq_scales = tile("wq_scales%d" % n, [P, PIECE], U8)
-            nc.vector.tensor_tensor(wq[:], w[:], qs_cols[:].unsqueeze(1).to_broadcast([P, PIECE, PACK]), ALU.mult)
-            quantise(wq_codes[:], wq_scales[:], wq[:].rearrange("p i r -> p (i r)"))
-            pair_bank = ps.tile([P, PACK, PIECE], F32, name="a_bank%d" % n)
-            for t in range(E // P):
+            quantise(wq_codes[:], wq_scales[:], wq_tiles[n][:])
+            dl_banks[n] = ps.tile([P, PACK, PIECE], F32, name="a_bank%d" % n)
+            for t in range(TILES):
                 rows = slice(t * P, (t + 1) * P)
-                nc.tensor.matmul_mx(
-                    out=pair_bank[:, t, :] if t < 2 else late_banks[t - 2][:, n * PIECE : (n + 1) * PIECE],
-                    lhsT=m_codes[:, rows].bitcast(FP8X4), lhsT_scale=m_scales[:, rows],
-                    rhs=wq_codes[:].bitcast(FP8X4), rhs_scale=wq_scales[:],
-                    start=True, stop=True,
-                )
-            dl = tile("dl%d" % n, [P, 2, PIECE], F32)
-            nc.scalar.copy(dl[:], pair_bank[:, 0:2, :])
-            places = place_list[:, n * OFFS_COLS : (n + 1) * OFFS_COLS]
-            for t in range(2):
-                nc.scalar.activation(windows[t][:].indirect(places), dl[:, t, :], ACT.Copy)
+                dst = dl_banks[n][:, t, :] if t < TILES - 1 else late_bank[:, n * PIECE : (n + 1) * PIECE]
+                product(dst, m_codes[:, rows].bitcast(FP8X4), m_scales[:, rows], wq_codes[:].bitcast(FP8X4), wq_scales[:])
 
-        late_banks = [ps.tile([P, I], F32, name="late_bank%d" % t) for t in range(2)]
-        quantise_notes(0)
+        def deliver(n, first, last, name):
+            dl = tile(name, [P, PIECE * (last - first)], F32)
+            nc.scalar.copy(dl[:], dl_banks[n][:, first:last, :].rearrange("p t i -> p (t i)"))
+            places = place_list[:, n * OFFS_COLS : (n + 1) * OFFS_COLS]
+            for t in range(first, last):
+                src = dl[:, (t - first) * PIECE : (t - first + 1) * PIECE]
+                nc.scalar.activation(windows[t][:].indirect(places), src, ACT.Copy)
+
+        def quantise_msgs(h):
+            cols = slice(h * (E // 2), (h + 1) * (E // 2))
+            quantise(m_codes[:, cols], m_scales[:, cols], m_grouped[:, h * 2 * E : (h + 1) * 2 * E])
+
+        group_notes(0)
         nc.vector.tensor_copy(q2_view[:, P // 2 : P], q2_halves[1][:].rearrange("p j (m r) -> p m j r", r=PACK))
+        quantise_notes(0)
         quantise(q2_codes[:], q2_scales[:], q2_grouped[:])
+        a_banks = [ps.tile([P, PACK, PIECE], F32, name="a_bank%d" % n) for n in range(PIECES)]
+        a_sb = [
+            shared.tile([P, PACK, PIECE], F32, name="a_sb%d" % n, offset=off, align_bytes=64)
+            for n, off in enumerate((0, 4096, 6144, 8192))
+        ]
+        for n in range(PIECES):
+            cols = slice(n * PIECE, (n + 1) * PIECE)
+            for r in range(PACK):
+                rows = slice(r * P, (r + 1) * P)
+                product(a_banks[n][:, r, :], q_codes[:, rows].bitcast(FP8X4), q_scales[:, rows],
+                        kg_words[:, cols].bitcast(FP4X4), kg_bytes[:, cols])
+            nc.scalar.copy(a_sb[n][:], a_banks[n][:])
+
+        for n in range(1, PIECES):
+            group_notes(n)
         for h in range(2):
             cols = slice(h * (E // 2), (h + 1) * (E // 2))
-            nc.gpsimd.tensor_scalar(
-                m_grouped[:, h * 2 * E : (h + 1) * 2 * E].rearrange("p (c i j) -> p c j i", i=4, j=PACK),
-                msgs_raw[:, :, cols].rearrange("p j (c i) -> p c j i", i=4),
-                1.0, 0.0, ALU.mult, ALU.add,
-            )
-        faded = [tile("faded%d" % t, [P, M], F32) for t in range(E // P)]
-        for n in range(PIECES):
-            w = scores(n)
-            if n == 0:
-                for h in range(2):
-                    cols = slice(h * (E // 2), (h + 1) * (E // 2))
-                    quantise(m_codes[:, cols], m_scales[:, cols], m_grouped[:, h * 2 * E : (h + 1) * 2 * E])
-            deliver(n, w)
-            if n + 1 < PIECES:
-                quantise_notes(n + 1)
+            dst = m_grouped[:, h * 2 * E : (h + 1) * 2 * E].rearrange("p (c i j) -> p c j i", i=4, j=PACK)
+            src = msgs_raw[:, :, cols].rearrange("p j (c i) -> p c j i", i=4)
+            if h == 0:
+                nc.scalar.copy(dst, src)
+            else:
+                nc.gpsimd.tensor_scalar(
+                    m_grouped[:, h * 2 * E : (h + 1) * 2 * E].rearrange("p (c j) -> p c j", j=PACK),
+                    msgs_raw[:, :, cols].rearrange("p j c -> p c j"),
+                    1.0, 0.0, ALU.mult, ALU.add,
+                )
 
-        late3 = tile("late3", [P, I], F32)
-        nc.vector.tensor_copy(late3[:], late_banks[1][:])
-        nc.vector.tensor_copy(windows[3][:].indirect(place_list[:]), late3[:])
-        late2 = tile("late2", [P, I], F32)
-        nc.scalar.copy(late2[:], late_banks[0][:])
-        for h in range(2):
-            nc.scalar.activation(
-                windows[2][:].indirect(place_list[:, 16 * h : 16 * h + 16]), late2[:, 256 * h : 256 * h + 256], ACT.Copy
-            )
+        take_smaller(0)
+        quantise_notes(1)
+        add_b(0)
+        take_smaller(1)
+        add_a(0)
+        add_b(1)
+        quantise_msgs(0)
+        weigh(0)
+        quantise_msgs(1)
+        messages(0)
+        add_a(1)
+        quantise_notes(2)
+        quantise_notes(3)
+        take_smaller(2)
+        weigh(1)
+        add_b(2)
+        messages(1)
+        deliver(0, 0, 1, "dl0")
+        add_a(2)
+        take_smaller(3)
+        deliver(0, 1, 3, "s_then_dl2")
+        weigh(2)
+        add_b(3)
+        messages(2)
+        add_a(3)
+        deliver(1, 0, 3, "s_then_dl3")
+        weigh(3)
+        messages(3)
+        deliver(2, 0, 3, "dl2")
+        deliver(3, 0, 3, "dl3")
 
-        for t in (0, 1, 3, 2):
-            for c in range(4):
-                cols = slice(c * (M // 4), (c + 1) * (M // 4))
+        late = tile("late", [P, I], F32)
+        nc.vector.tensor_copy(late[:], late_bank[:])
+        nc.vector.tensor_copy(windows[TILES - 1][:].indirect(place_list[:]), late[:])
+
+        faded = [tile("faded%d" % t, [P, M], F32) for t in range(TILES)]
+        for t in order:
+            for c in range(FADE_CUTS):
+                cols = slice(c * (M // FADE_CUTS), (c + 1) * (M // FADE_CUTS))
                 nc.gpsimd.tensor_tensor(faded[t][:, cols], old_tiles[t][:, cols], fade_rows[:, cols], ALU.mult)
-        for t in (0, 1, 3, 2):
+        for t in order:
             res = tile("res%d" % t, [P, M], F32)
-            cuts = 2 if t == 2 else 1
+            cuts = 2 if t == order[-1] else 1
             for c in range(cuts):
                 cols = slice(c * (M // cuts), (c + 1) * (M // cuts))
                 nc.vector.tensor_tensor(res[:, cols], faded[t][:, cols], windows[t][:, cols], ALU.add)

@@ -23,8 +23,10 @@ PIECE = 128
 PIECES = I // PIECE
 OFFS_COLS = PIECE // 16
 TILES = E // P
+EARLY = 2
+VECTOR_SLOTS = 128
 FADE_COLS = M // P
-FADE_CUTS = 4
+FADE_CUTS = 2
 
 
 def tile_attend_twopools_delivered_lean_kernel(
@@ -65,7 +67,6 @@ def tile_attend_twopools_delivered_lean_kernel(
         ident = tile("ident", [P, P], F32)
 
         make_identity(nc, ident[:])
-        nc.gpsimd.dma_start(lam_cols[:], lam.rearrange("(p r) o -> p (r o)", r=PACK))
         nc.sync.dma_start(qs_cols[:], qs.rearrange("(p r) o -> p (r o)", r=PACK))
         nc.sync.dma_start(fade_cols[:], fade.rearrange("o (p c) -> p (o c)", c=FADE_COLS))
         warm = tile("warm", [P, 1], F32)
@@ -89,14 +90,15 @@ def tile_attend_twopools_delivered_lean_kernel(
             nc.sync.dma_start(
                 q2_halves[h][:], query2.rearrange("(p j) c -> p j c", j=PACK)[:, :, h * (Q // 2) : (h + 1) * (Q // 2)]
             )
+        nc.sync.dma_start(lam_cols[:], lam.rearrange("(p r) o -> p (r o)", r=PACK))
         nc.sync.dma_start(msgs_raw[:], msgs.rearrange("(p j) c -> p j c", j=PACK))
         nc.sync.dma_start(place_list[:], offs3)
-        order = [TILES - 1] + list(range(TILES - 1))
+        order = list(range(TILES))
         for t in order:
             nc.sync.dma_start(old_tiles[t][:], old[t * P : (t + 1) * P, :])
 
         for t in range(TILES):
-            nc.vector.memset(windows[t][:], 0.0) if t < 2 else nc.gpsimd.memset(windows[t][:], 0.0)
+            nc.vector.memset(windows[t][:], 0.0)
 
         qs_rows_bank = ps.tile([P, PACK, P], F32, name="b_bank", bufs=2)
         for r in range(PACK):
@@ -123,19 +125,18 @@ def tile_attend_twopools_delivered_lean_kernel(
         q_grouped = tile("q_grouped", [P, Q * PACK], BF16)
         q_codes = tile("q_codes", [P, Q], U32)
         q_scales = tile("q_scales", [P, Q], U8)
-        nc.gpsimd.tensor_scalar(
-            q_grouped[:].rearrange("p (r m j) -> p r m j", r=PACK, j=PACK),
-            q_raw[:].rearrange("p j (m r) -> p r m j", r=PACK),
-            1.0, 0.0, ALU.mult, ALU.add,
+        nc.vector.tensor_copy(
+            q_grouped[:].rearrange("p (r m j) -> p m j r", r=PACK, j=PACK),
+            q_raw[:].rearrange("p j (m r) -> p m j r", r=PACK),
         )
-        nc.vector.tensor_copy(kg_bytes[:], key_bytes[:].indirect(key_list[:]))
         quantise(q_codes[:], q_scales[:], q_grouped[:])
+        nc.vector.tensor_copy(kg_bytes[:], key_bytes[:].indirect(key_list[:]))
         lam_less_one = tile("lam_less_one", [P, PACK], F32)
-        nc.gpsimd.tensor_scalar(lam_less_one[:], lam_cols[:], 1.0, -1.0, ALU.mult, ALU.add)
+        nc.vector.tensor_scalar(lam_less_one[:], lam_cols[:], -1.0, None, ALU.add)
 
         ng_all = tile("ng_all", [P, PACK, I], BF16)
         for j in range(PACK):
-            if j == 2:
+            if j % 2 == 0:
                 nc.scalar.activation(ng_all[:, j, :], note_planes[j][:].indirect(note_list[:]), ACT.Copy)
             else:
                 nc.vector.tensor_copy(ng_all[:, j, :], note_planes[j][:].indirect(note_list[:]))
@@ -173,7 +174,6 @@ def tile_attend_twopools_delivered_lean_kernel(
         m_scales = tile("m_scales", [P, E], U8)
 
         b_banks, smaller, part, w_tiles, wq_tiles, dl_banks = {}, {}, {}, {}, {}, {}
-        late_bank = ps.tile([P, I], F32, name="late_bank")
 
         def take_smaller(n):
             cols = slice(n * PIECE, (n + 1) * PIECE)
@@ -197,12 +197,13 @@ def tile_attend_twopools_delivered_lean_kernel(
             s = tile("s_then_dl%d" % n, [P, PIECE * PACK], F32)
             w_tiles[n] = tile("w%d" % n, [P, PIECE * PACK], F32)
             nc.vector.tensor_tensor(
-                s[:].rearrange("p (c i r) -> p c r i", i=4, r=PACK),
-                part[n][:].rearrange("p r (c i) -> p c r i", i=4),
-                a_banks[n][:].rearrange("p r (c i) -> p c r i", i=4),
-                ALU.add,
+                s[:], part[n][:].rearrange("p r i -> p (r i)"), a_banks[n][:].rearrange("p r i -> p (r i)"), ALU.add
             )
-            nc.scalar.activation(w_tiles[n][:], s[:], ACT.Sigmoid)
+            nc.scalar.activation(
+                w_tiles[n][:].rearrange("p (c i r) -> p c r i", i=4, r=PACK),
+                s[:].rearrange("p (r c i) -> p c r i", i=4, r=PACK),
+                ACT.Sigmoid,
+            )
 
         def weigh(n):
             wq_tiles[n] = tile("wq%d" % n, [P, PIECE * PACK], BF16)
@@ -213,23 +214,24 @@ def tile_attend_twopools_delivered_lean_kernel(
                 ALU.mult,
             )
 
-        def messages(n):
-            wq_codes = tile("wq_codes%d" % n, [P, PIECE], U32)
-            wq_scales = tile("wq_scales%d" % n, [P, PIECE], U8)
-            quantise(wq_codes[:], wq_scales[:], wq_tiles[n][:])
-            dl_banks[n] = ps.tile([P, PACK, PIECE], F32, name="a_bank%d" % n)
-            for t in range(TILES):
-                rows = slice(t * P, (t + 1) * P)
-                dst = dl_banks[n][:, t, :] if t < TILES - 1 else late_bank[:, n * PIECE : (n + 1) * PIECE]
-                product(dst, m_codes[:, rows].bitcast(FP8X4), m_scales[:, rows], wq_codes[:].bitcast(FP8X4), wq_scales[:])
+        wq_codes = tile("wq_codes", [P, I], U32)
+        wq_scales = tile("wq_scales", [P, I], U8)
 
-        def deliver(n, first, last, name):
-            dl = tile(name, [P, PIECE * (last - first)], F32)
-            nc.scalar.copy(dl[:], dl_banks[n][:, first:last, :].rearrange("p t i -> p (t i)"))
+        def messages(n):
+            cols = slice(n * PIECE, (n + 1) * PIECE)
+            quantise(wq_codes[:, cols], wq_scales[:, cols], wq_tiles[n][:])
+            dl_banks[n] = ps.tile([P, PACK, PIECE], F32, name="a_bank%d" % n)
+            for t in range(EARLY):
+                rows = slice(t * P, (t + 1) * P)
+                product(dl_banks[n][:, t, :], m_codes[:, rows].bitcast(FP8X4), m_scales[:, rows],
+                        wq_codes[:, cols].bitcast(FP8X4), wq_scales[:, cols])
+
+        def deliver(n):
+            dl = tile("s_then_dl%d" % (n + 1), [P, PIECE * EARLY], F32)
+            nc.scalar.copy(dl[:], dl_banks[n][:, 0:EARLY, :].rearrange("p t i -> p (t i)"))
             places = place_list[:, n * OFFS_COLS : (n + 1) * OFFS_COLS]
-            for t in range(first, last):
-                src = dl[:, (t - first) * PIECE : (t - first + 1) * PIECE]
-                nc.scalar.activation(windows[t][:].indirect(places), src, ACT.Copy)
+            for t in range(EARLY):
+                nc.scalar.activation(windows[t][:].indirect(places), dl[:, t * PIECE : (t + 1) * PIECE], ACT.Copy)
 
         def quantise_msgs(h):
             cols = slice(h * (E // 2), (h + 1) * (E // 2))
@@ -258,14 +260,7 @@ def tile_attend_twopools_delivered_lean_kernel(
             cols = slice(h * (E // 2), (h + 1) * (E // 2))
             dst = m_grouped[:, h * 2 * E : (h + 1) * 2 * E].rearrange("p (c i j) -> p c j i", i=4, j=PACK)
             src = msgs_raw[:, :, cols].rearrange("p j (c i) -> p c j i", i=4)
-            if h == 0:
-                nc.scalar.copy(dst, src)
-            else:
-                nc.gpsimd.tensor_scalar(
-                    m_grouped[:, h * 2 * E : (h + 1) * 2 * E].rearrange("p (c j) -> p c j", j=PACK),
-                    msgs_raw[:, :, cols].rearrange("p j c -> p c j"),
-                    1.0, 0.0, ALU.mult, ALU.add,
-                )
+            nc.scalar.copy(dst, src)
 
         take_smaller(0)
         quantise_notes(1)
@@ -275,38 +270,50 @@ def tile_attend_twopools_delivered_lean_kernel(
         add_b(1)
         quantise_msgs(0)
         weigh(0)
-        quantise_msgs(1)
-        messages(0)
-        add_a(1)
-        quantise_notes(2)
-        quantise_notes(3)
-        take_smaller(2)
-        weigh(1)
-        add_b(2)
-        messages(1)
-        deliver(0, 0, 1, "dl0")
-        add_a(2)
-        take_smaller(3)
-        deliver(0, 1, 3, "s_then_dl2")
-        weigh(2)
-        add_b(3)
-        messages(2)
-        add_a(3)
-        deliver(1, 0, 3, "s_then_dl3")
-        weigh(3)
-        messages(3)
-        deliver(2, 0, 3, "dl2")
-        deliver(3, 0, 3, "dl3")
+        for n in range(PIECES):
+            messages(n)
+            if n == 0:
+                quantise_notes(2)
+            if n + 1 < PIECES:
+                add_a(n + 1)
+            if n == 0:
+                quantise_notes(3)
+            if n + 2 < PIECES:
+                take_smaller(n + 2)
+            if n == 1:
+                quantise_msgs(1)
+            deliver(n)
+            if n + 1 < PIECES:
+                weigh(n + 1)
+            if n + 2 < PIECES:
+                add_b(n + 2)
 
-        late = tile("late", [P, I], F32)
-        nc.vector.tensor_copy(late[:], late_bank[:])
-        nc.vector.tensor_copy(windows[TILES - 1][:].indirect(place_list[:]), late[:])
+        late = {}
+        for t in range(EARLY, TILES):
+            rows = slice(t * P, (t + 1) * P)
+            bank = ps.tile([P, I], F32, name="b_bank", bufs=2)
+            product(bank[:], m_codes[:, rows].bitcast(FP8X4), m_scales[:, rows], wq_codes[:].bitcast(FP8X4), wq_scales[:])
+            late[t] = tile("late%d" % t, [P, I], F32)
+            if t < TILES - 1:
+                nc.scalar.copy(late[t][:], bank[:])
+                for h in range(2):
+                    nc.scalar.activation(
+                        windows[t][:].indirect(place_list[:, 16 * h : 16 * h + 16]), late[t][:, 256 * h : 256 * h + 256], ACT.Copy
+                    )
+            else:
+                nc.vector.tensor_copy(late[t][:], bank[:])
+                nc.vector.tensor_copy(
+                    windows[t][:].indirect(place_list[:, 0 : VECTOR_SLOTS // 16]), late[t][:, 0:VECTOR_SLOTS]
+                )
+                nc.scalar.activation(
+                    windows[t][:].indirect(place_list[:, VECTOR_SLOTS // 16 :]), late[t][:, VECTOR_SLOTS:], ACT.Copy
+                )
 
         faded = [tile("faded%d" % t, [P, M], F32) for t in range(TILES)]
         for t in order:
             for c in range(FADE_CUTS):
                 cols = slice(c * (M // FADE_CUTS), (c + 1) * (M // FADE_CUTS))
-                nc.gpsimd.tensor_tensor(faded[t][:, cols], old_tiles[t][:, cols], fade_rows[:, cols], ALU.mult)
+                nc.vector.tensor_tensor(faded[t][:, cols], old_tiles[t][:, cols], fade_rows[:, cols], ALU.mult)
         for t in order:
             res = tile("res%d" % t, [P, M], F32)
             cuts = 2 if t == order[-1] else 1

@@ -23,8 +23,7 @@ PIECE = 128
 PIECES = I // PIECE
 OFFS_COLS = PIECE // 16
 TILES = E // P
-EARLY = 2
-VECTOR_SLOTS = 128
+SPLIT = 320
 FADE_COLS = M // P
 FADE_CUTS = 2
 
@@ -67,22 +66,21 @@ def tile_attend_twopools_delivered_lean_kernel(
         ident = tile("ident", [P, P], F32)
 
         make_identity(nc, ident[:])
-        nc.sync.dma_start(qs_cols[:], qs.rearrange("(p r) o -> p (r o)", r=PACK))
-        nc.sync.dma_start(fade_cols[:], fade.rearrange("o (p c) -> p (o c)", c=FADE_COLS))
         warm = tile("warm", [P, 1], F32)
         nc.scalar.activation(warm[:], ident[:, 0:1], ACT.Sigmoid)
 
+        nc.sync.dma_start(fade_cols[:], fade.rearrange("o (p c) -> p (o c)", c=FADE_COLS))
         nc.vector.memset(key_bytes[:].bitcast(I32), 0)
         nc.sync.dma_start(key_words[:].bitcast(I32), keys_words[0].bitcast(I32))
         nc.sync.dma_start(key_list[:], offs)
-        nc.sync.dma_start(q_raw[:], query.rearrange("(p j) c -> p j c", j=PACK))
-        notes_by_plane = notes.rearrange("(p j) u -> p j u", j=PACK)
-        nc.sync.dma_start(note_planes[0][:], notes_by_plane[:, 0, :])
         for quad in range(4):
             nc.sync.dma_start(
                 key_bytes[32 * quad : 32 * quad + 4, :].bitcast(I32),
                 keys_scales[0, 4 * quad : 4 * quad + 4, :].bitcast(I32),
             )
+        nc.sync.dma_start(q_raw[:], query.rearrange("(p j) c -> p j c", j=PACK))
+        notes_by_plane = notes.rearrange("(p j) u -> p j u", j=PACK)
+        nc.sync.dma_start(note_planes[0][:], notes_by_plane[:, 0, :])
         nc.sync.dma_start(note_list[:], offs2)
         for j in range(1, PACK):
             nc.sync.dma_start(note_planes[j][:], notes_by_plane[:, j, :])
@@ -92,25 +90,18 @@ def tile_attend_twopools_delivered_lean_kernel(
             )
         nc.sync.dma_start(lam_cols[:], lam.rearrange("(p r) o -> p (r o)", r=PACK))
         nc.sync.dma_start(msgs_raw[:], msgs.rearrange("(p j) c -> p j c", j=PACK))
+        nc.sync.dma_start(qs_cols[:], qs.rearrange("(p r) o -> p (r o)", r=PACK))
         nc.sync.dma_start(place_list[:], offs3)
-        order = list(range(TILES))
+        order = range(TILES)
         for t in order:
             nc.sync.dma_start(old_tiles[t][:], old[t * P : (t + 1) * P, :])
 
         for t in range(TILES):
             nc.vector.memset(windows[t][:], 0.0)
 
-        qs_rows_bank = ps.tile([P, PACK, P], F32, name="b_bank", bufs=2)
-        for r in range(PACK):
-            nc.tensor.transpose(qs_rows_bank[:, r, :], qs_cols[:, r : r + 1].to_broadcast([P, P]), ident[:])
-        qs_rows = tile("qs_rows", [P, PACK, P], F32)
-        nc.scalar.copy(qs_rows[:], qs_rows_bank[:])
-        qs_bank = ps.tile([P, PACK, PIECE], F32, name="qs_bank")
-        for r in range(PACK):
-            nc.tensor.transpose(qs_bank[:, r, :], qs_rows[:, r, :], ident[:])
         fade_rows = tile("fade_rows", [P, M], F32)
         for h in range(2):
-            fade_bank = ps.tile([P, 4, P], F32, name="b_bank", bufs=2)
+            fade_bank = ps.tile([P, 4, P], F32, name="fade_bank%d" % h)
             for c in range(4):
                 col = 4 * h + c
                 nc.tensor.transpose(fade_bank[:, c, :], fade_cols[:, col : col + 1].to_broadcast([P, P]), ident[:])
@@ -136,7 +127,7 @@ def tile_attend_twopools_delivered_lean_kernel(
 
         ng_all = tile("ng_all", [P, PACK, I], BF16)
         for j in range(PACK):
-            if j % 2 == 0:
+            if j == 0:
                 nc.scalar.activation(ng_all[:, j, :], note_planes[j][:].indirect(note_list[:]), ACT.Copy)
             else:
                 nc.vector.tensor_copy(ng_all[:, j, :], note_planes[j][:].indirect(note_list[:]))
@@ -150,24 +141,21 @@ def tile_attend_twopools_delivered_lean_kernel(
         n_codes = tile("n_codes", [P, I], U32)
         n_scales = tile("n_scales", [P, I], U8)
 
-        n_grouped = [
-            shared.tile([P, PIECE * PACK], BF16, name="n_grouped%d" % n, offset=off, align_bytes=64)
-            for n, off in enumerate((10240, 2048, 3072, 11264))
-        ]
+        n_grouped = [tile("n_grouped0", [P, PIECE * PACK], BF16)]
+        n_grouped.append(shared.tile([P, PIECE * PACK], BF16, name="n_grouped1", offset=0, align_bytes=64))
+        n_grouped.append(shared.tile([P, 2 * PIECE * PACK], BF16, name="n_grouped2", offset=2048, align_bytes=64))
+        note_cols = [slice(0, PIECE), slice(PIECE, 2 * PIECE), slice(2 * PIECE, I)]
 
         def group_notes(n):
-            cols = slice(n * PIECE, (n + 1) * PIECE)
-            grouped = n_grouped[n]
-            dst = grouped[:].rearrange("p (c i j) -> p c j i", i=4, j=PACK)
-            src = ng_all[:, :, cols].rearrange("p j (c i) -> p c j i", i=4)
+            dst = n_grouped[n][:].rearrange("p (c i j) -> p c j i", i=4, j=PACK)
+            src = ng_all[:, :, note_cols[n]].rearrange("p j (c i) -> p c j i", i=4)
             if n == 0:
                 nc.vector.tensor_copy(dst, src)
             else:
                 nc.scalar.copy(dst, src)
 
         def quantise_notes(n):
-            cols = slice(n * PIECE, (n + 1) * PIECE)
-            quantise(n_codes[:, cols], n_scales[:, cols], n_grouped[n][:])
+            quantise(n_codes[:, note_cols[n]], n_scales[:, note_cols[n]], n_grouped[n][:])
 
         m_grouped = tile("m_grouped", [P, E * PACK], BF16)
         m_codes = tile("m_codes", [P, E], U32)
@@ -210,28 +198,28 @@ def tile_attend_twopools_delivered_lean_kernel(
             nc.vector.tensor_tensor(
                 wq_tiles[n][:].rearrange("p (i r) -> p i r", r=PACK),
                 w_tiles[n][:].rearrange("p (i r) -> p i r", r=PACK),
-                qs_bank[:].rearrange("p r i -> p i r"),
+                qs_cols[:].unsqueeze(1).to_broadcast([P, PIECE, PACK]),
                 ALU.mult,
             )
 
         wq_codes = tile("wq_codes", [P, I], U32)
         wq_scales = tile("wq_scales", [P, I], U8)
 
-        def messages(n):
+        def messages(n, tiles):
             cols = slice(n * PIECE, (n + 1) * PIECE)
             quantise(wq_codes[:, cols], wq_scales[:, cols], wq_tiles[n][:])
             dl_banks[n] = ps.tile([P, PACK, PIECE], F32, name="a_bank%d" % n)
-            for t in range(EARLY):
+            for place, t in enumerate(tiles):
                 rows = slice(t * P, (t + 1) * P)
-                product(dl_banks[n][:, t, :], m_codes[:, rows].bitcast(FP8X4), m_scales[:, rows],
+                product(dl_banks[n][:, place, :], m_codes[:, rows].bitcast(FP8X4), m_scales[:, rows],
                         wq_codes[:, cols].bitcast(FP8X4), wq_scales[:, cols])
 
-        def deliver(n):
-            dl = tile("s_then_dl%d" % (n + 1), [P, PIECE * EARLY], F32)
-            nc.scalar.copy(dl[:], dl_banks[n][:, 0:EARLY, :].rearrange("p t i -> p (t i)"))
+        def deliver(n, first, name):
+            dl = tile(name, [P, PIECE * 2], F32)
+            nc.scalar.copy(dl[:], dl_banks[n][:, first : first + 2, :].rearrange("p t i -> p (t i)"))
             places = place_list[:, n * OFFS_COLS : (n + 1) * OFFS_COLS]
-            for t in range(EARLY):
-                nc.scalar.activation(windows[t][:].indirect(places), dl[:, t * PIECE : (t + 1) * PIECE], ACT.Copy)
+            for k in range(2):
+                nc.scalar.activation(windows[first + k][:].indirect(places), dl[:, k * PIECE : (k + 1) * PIECE], ACT.Copy)
 
         def quantise_msgs(h):
             cols = slice(h * (E // 2), (h + 1) * (E // 2))
@@ -240,11 +228,13 @@ def tile_attend_twopools_delivered_lean_kernel(
         group_notes(0)
         nc.vector.tensor_copy(q2_view[:, P // 2 : P], q2_halves[1][:].rearrange("p j (m r) -> p m j r", r=PACK))
         quantise_notes(0)
-        quantise(q2_codes[:], q2_scales[:], q2_grouped[:])
+        for r in range(PACK):
+            rows = slice(r * P, (r + 1) * P)
+            quantise(q2_codes[:, rows], q2_scales[:, rows], q2_grouped[:, r * Q : (r + 1) * Q])
         a_banks = [ps.tile([P, PACK, PIECE], F32, name="a_bank%d" % n) for n in range(PIECES)]
         a_sb = [
             shared.tile([P, PACK, PIECE], F32, name="a_sb%d" % n, offset=off, align_bytes=64)
-            for n, off in enumerate((0, 4096, 6144, 8192))
+            for n, off in enumerate((8192, 10240, 12288, 4096))
         ]
         for n in range(PIECES):
             cols = slice(n * PIECE, (n + 1) * PIECE)
@@ -254,8 +244,8 @@ def tile_attend_twopools_delivered_lean_kernel(
                         kg_words[:, cols].bitcast(FP4X4), kg_bytes[:, cols])
             nc.scalar.copy(a_sb[n][:], a_banks[n][:])
 
-        for n in range(1, PIECES):
-            group_notes(n)
+        group_notes(1)
+        group_notes(2)
         for h in range(2):
             cols = slice(h * (E // 2), (h + 1) * (E // 2))
             dst = m_grouped[:, h * 2 * E : (h + 1) * 2 * E].rearrange("p (c i j) -> p c j i", i=4, j=PACK)
@@ -265,49 +255,56 @@ def tile_attend_twopools_delivered_lean_kernel(
         take_smaller(0)
         quantise_notes(1)
         add_b(0)
-        take_smaller(1)
         add_a(0)
-        add_b(1)
         quantise_msgs(0)
+        take_smaller(1)
         weigh(0)
-        for n in range(PIECES):
-            messages(n)
-            if n == 0:
-                quantise_notes(2)
-            if n + 1 < PIECES:
-                add_a(n + 1)
-            if n == 0:
-                quantise_notes(3)
-            if n + 2 < PIECES:
-                take_smaller(n + 2)
-            if n == 1:
-                quantise_msgs(1)
-            deliver(n)
-            if n + 1 < PIECES:
-                weigh(n + 1)
-            if n + 2 < PIECES:
-                add_b(n + 2)
+        quantise_msgs(1)
+        messages(0, (0, 1, 2, 3))
+        add_b(1)
+        quantise_notes(2)
+        add_a(1)
+        deliver(0, 0, "dl0")
+        take_smaller(2)
+        deliver(0, 2, "s_then_dl1")
+        weigh(1)
+        add_b(2)
+        messages(1, (0, 1))
+        add_a(2)
+        take_smaller(3)
+        deliver(1, 0, "s_then_dl2")
+        weigh(2)
+        add_b(3)
+        messages(2, (0, 1))
+        add_a(3)
+        deliver(2, 0, "s_then_dl3")
+        weigh(3)
+        messages(3, (0, 1))
+        deliver(3, 0, "dl3")
 
-        late = {}
-        for t in range(EARLY, TILES):
+        def late_product(bank, t, lo, hi):
             rows = slice(t * P, (t + 1) * P)
-            bank = ps.tile([P, I], F32, name="b_bank", bufs=2)
-            product(bank[:], m_codes[:, rows].bitcast(FP8X4), m_scales[:, rows], wq_codes[:].bitcast(FP8X4), wq_scales[:])
-            late[t] = tile("late%d" % t, [P, I], F32)
-            if t < TILES - 1:
-                nc.scalar.copy(late[t][:], bank[:])
-                for h in range(2):
-                    nc.scalar.activation(
-                        windows[t][:].indirect(place_list[:, 16 * h : 16 * h + 16]), late[t][:, 256 * h : 256 * h + 256], ACT.Copy
-                    )
+            product(bank[:, lo:hi], m_codes[:, rows].bitcast(FP8X4), m_scales[:, rows],
+                    wq_codes[:, lo:hi].bitcast(FP8X4), wq_scales[:, lo:hi])
+
+        def late_deliver(engine, bank, t, lo, hi):
+            late = tile("late%d_%d" % (t, lo), [P, hi - lo], F32)
+            target = windows[t][:].indirect(place_list[:, lo // 16 : hi // 16])
+            if engine == "vector":
+                nc.vector.tensor_copy(late[:], bank[:, lo:hi])
+                nc.vector.tensor_copy(target, late[:])
             else:
-                nc.vector.tensor_copy(late[t][:], bank[:])
-                nc.vector.tensor_copy(
-                    windows[t][:].indirect(place_list[:, 0 : VECTOR_SLOTS // 16]), late[t][:, 0:VECTOR_SLOTS]
-                )
-                nc.scalar.activation(
-                    windows[t][:].indirect(place_list[:, VECTOR_SLOTS // 16 :]), late[t][:, VECTOR_SLOTS:], ACT.Copy
-                )
+                nc.scalar.copy(late[:], bank[:, lo:hi])
+                nc.scalar.activation(target, late[:], ACT.Copy)
+
+        banks = {}
+        for t in (3, 2):
+            banks[t] = ps.tile([P, I], F32, name="b_bank", bufs=2)
+            late_product(banks[t], t, 2 * PIECE, I)
+            late_product(banks[t], t, PIECE, 2 * PIECE)
+        late_deliver("vector", banks[3], 3, SPLIT, I)
+        late_deliver("scalar", banks[2], 2, PIECE, I)
+        late_deliver("scalar", banks[3], 3, PIECE, SPLIT)
 
         faded = [tile("faded%d" % t, [P, M], F32) for t in range(TILES)]
         for t in order:
@@ -316,8 +313,7 @@ def tile_attend_twopools_delivered_lean_kernel(
                 nc.vector.tensor_tensor(faded[t][:, cols], old_tiles[t][:, cols], fade_rows[:, cols], ALU.mult)
         for t in order:
             res = tile("res%d" % t, [P, M], F32)
-            cuts = 2 if t == order[-1] else 1
-            for c in range(cuts):
-                cols = slice(c * (M // cuts), (c + 1) * (M // cuts))
-                nc.vector.tensor_tensor(res[:, cols], faded[t][:, cols], windows[t][:, cols], ALU.add)
-                nc.sync.dma_start(out[t * P : (t + 1) * P, cols], res[:, cols])
+            edges = (0, M // 2, 3 * M // 4, M) if t == order[-1] else (0, M)
+            for lo, hi in zip(edges, edges[1:]):
+                nc.vector.tensor_tensor(res[:, lo:hi], faded[t][:, lo:hi], windows[t][:, lo:hi], ALU.add)
+                nc.sync.dma_start(out[t * P : (t + 1) * P, lo:hi], res[:, lo:hi])

from contextlib import ExitStack

import concourse.mybir as mybir
from concourse.masks import make_identity

D, T, I, Q, E, U, M = 512, 2048, 512, 512, 512, 1024, 1024
FLOPS = 3 * 2 * 512 * 512 * 512

F32 = mybir.dt.float32
BF16 = mybir.dt.bfloat16
I32 = mybir.dt.int32
U32 = mybir.dt.uint32
U16 = mybir.dt.uint16
U8 = mybir.dt.uint8
FP8X4 = mybir.dt.float8_e4m3fn_x4
FP4X4 = mybir.dt.float4_e2m1fn_x4
ALU = mybir.AluOpType
ACT = mybir.ActivationFunctionType

P = 128
PACK = 4
PIECE = 128
PIECES = I // PIECE
OFFS_COLS = PIECE // 16
TILES = E // P
SPLIT = 320
FADE_COLS = M // P
FADE_CUTS = 2


def tile_attend_twopools_delivered_lean_kernel(
    tc, query, keys_words, keys_scales, query2, notes, lam, qs, msgs, old, fade, offs, offs2, offs3, out
):
    nc = tc.nc
    with ExitStack() as ctx:
        sb = ctx.enter_context(tc.tile_pool(name="sb", bufs=1))
        shared = ctx.enter_context(tc.tile_pool(name="shared", bufs=1))
        ps = ctx.enter_context(tc.psum_pool(name="ps", bufs=1))

        def tile(name, shape, dtype):
            return sb.tile(shape, dtype, name=name, align_bytes=64)

        def quantise(codes, scales, grouped):
            nc.vector.quantize_mx(out=codes.bitcast(FP8X4), scales=scales, in_=grouped)

        def product(dst, stat_codes, stat_scales, mov_codes, mov_scales):
            nc.tensor.matmul_mx(
                out=dst, lhsT=stat_codes, lhsT_scale=stat_scales, rhs=mov_codes, rhs_scale=mov_scales,
                start=True, stop=True,
            )

        key_list = tile("key_list", [P, I // 16], U16)
        note_list = tile("note_list", [P, I // 16], U16)
        place_list = tile("place_list", [P, I // 16], U16)
        key_words = tile("key_words", [P, T], U16)
        key_bytes = tile("key_bytes", [P, T], U8)
        q_raw = tile("q_raw", [P, PACK, Q], F32)
        q2_halves = [shared.tile([P, PACK, Q // 2], F32, name="q2_raw%d" % h, offset=4096 * h, align_bytes=64) for h in range(2)]
        msgs_raw = tile("msgs_raw", [P, PACK, E], F32)
        note_planes = [tile("note_plane%d" % j, [P, U], F32) for j in range(PACK)]
        old_tiles = [tile("old%d" % t, [P, M], F32) for t in range(TILES)]
        fade_cols = tile("fade_cols", [P, FADE_COLS], F32)
        lam_cols = tile("lam_cols", [P, PACK], F32)
        qs_cols = tile("qs_cols", [P, PACK], F32)
        windows = [tile("window%d" % t, [P, M], F32) for t in range(TILES)]
        ident = tile("ident", [P, P], F32)

        make_identity(nc, ident[:])
        warm = tile("warm", [P, 1], F32)
        nc.scalar.activation(warm[:], ident[:, 0:1], ACT.Sigmoid)

        nc.sync.dma_start(fade_cols[:], fade.rearrange("o (p c) -> p (o c)", c=FADE_COLS))
        nc.vector.memset(key_bytes[:].bitcast(I32), 0)
        nc.sync.dma_start(key_words[:].bitcast(I32), keys_words[0].bitcast(I32))
        nc.sync.dma_start(key_list[:], offs)
        for quad in range(4):
            nc.sync.dma_start(
                key_bytes[32 * quad : 32 * quad + 4, :].bitcast(I32),
                keys_scales[0, 4 * quad : 4 * quad + 4, :].bitcast(I32),
            )
        nc.sync.dma_start(q_raw[:], query.rearrange("(p j) c -> p j c", j=PACK))
        notes_by_plane = notes.rearrange("(p j) u -> p j u", j=PACK)
        nc.sync.dma_start(note_planes[0][:], notes_by_plane[:, 0, :])
        nc.sync.dma_start(note_list[:], offs2)
        for j in range(1, PACK):
            nc.sync.dma_start(note_planes[j][:], notes_by_plane[:, j, :])
        for h in range(2):
            nc.sync.dma_start(
                q2_halves[h][:], query2.rearrange("(p j) c -> p j c", j=PACK)[:, :, h * (Q // 2) : (h + 1) * (Q // 2)]
            )
        nc.sync.dma_start(lam_cols[:], lam.rearrange("(p r) o -> p (r o)", r=PACK))
        nc.sync.dma_start(msgs_raw[:], msgs.rearrange("(p j) c -> p j c", j=PACK))
        nc.sync.dma_start(qs_cols[:], qs.rearrange("(p r) o -> p (r o)", r=PACK))
        nc.sync.dma_start(place_list[:], offs3)
        order = range(TILES)
        for t in order:
            nc.sync.dma_start(old_tiles[t][:], old[t * P : (t + 1) * P, :])

        for t in range(TILES):
            nc.vector.memset(windows[t][:], 0.0)

        fade_rows = tile("fade_rows", [P, M], F32)
        for h in range(2):
            fade_bank = ps.tile([P, 4, P], F32, name="fade_bank%d" % h)
            for c in range(4):
                col = 4 * h + c
                nc.tensor.transpose(fade_bank[:, c, :], fade_cols[:, col : col + 1].to_broadcast([P, P]), ident[:])
            nc.scalar.copy(
                fade_rows[:].rearrange("p (n c) -> p n c", c=FADE_COLS)[:, :, 4 * h : 4 * h + 4],
                fade_bank[:].rearrange("p c n -> p n c"),
            )

        kg_words = tile("kg_words", [P, I], U16)
        kg_bytes = tile("kg_bytes", [P, I], U8)
        nc.vector.tensor_copy(kg_words[:], key_words[:].indirect(key_list[:]))
        q_grouped = tile("q_grouped", [P, Q * PACK], BF16)
        q_codes = tile("q_codes", [P, Q], U32)
        q_scales = tile("q_scales", [P, Q], U8)
        nc.vector.tensor_copy(
            q_grouped[:].rearrange("p (r m j) -> p m j r", r=PACK, j=PACK),
            q_raw[:].rearrange("p j (m r) -> p m j r", r=PACK),
        )
        quantise(q_codes[:], q_scales[:], q_grouped[:])
        nc.vector.tensor_copy(kg_bytes[:], key_bytes[:].indirect(key_list[:]))
        lam_less_one = tile("lam_less_one", [P, PACK], F32)
        nc.vector.tensor_scalar(lam_less_one[:], lam_cols[:], -1.0, None, ALU.add)

        ng_all = tile("ng_all", [P, PACK, I], BF16)
        for j in range(PACK):
            if j == 0:
                nc.scalar.activation(ng_all[:, j, :], note_planes[j][:].indirect(note_list[:]), ACT.Copy)
            else:
                nc.vector.tensor_copy(ng_all[:, j, :], note_planes[j][:].indirect(note_list[:]))

        q2_grouped = tile("q2_grouped", [P, Q * PACK], BF16)
        q2_codes = tile("q2_codes", [P, Q], U32)
        q2_scales = tile("q2_scales", [P, Q], U8)
        q2_view = q2_grouped[:].rearrange("p (r m j) -> p m j r", r=PACK, j=PACK)
        nc.scalar.copy(q2_view[:, 0 : P // 2], q2_halves[0][:].rearrange("p j (m r) -> p m j r", r=PACK))

        n_codes = tile("n_codes", [P, I], U32)
        n_scales = tile("n_scales", [P, I], U8)

        n_grouped = [tile("n_grouped0", [P, PIECE * PACK], BF16)]
        n_grouped.append(shared.tile([P, PIECE * PACK], BF16, name="n_grouped1", offset=0, align_bytes=64))
        n_grouped.append(shared.tile([P, 2 * PIECE * PACK], BF16, name="n_grouped2", offset=2048, align_bytes=64))
        note_cols = [slice(0, PIECE), slice(PIECE, 2 * PIECE), slice(2 * PIECE, I)]

        def group_notes(n):
            dst = n_grouped[n][:].rearrange("p (c i j) -> p c j i", i=4, j=PACK)
            src = ng_all[:, :, note_cols[n]].rearrange("p j (c i) -> p c j i", i=4)
            if n == 0:
                nc.vector.tensor_copy(dst, src)
            else:
                nc.scalar.copy(dst, src)

        def quantise_notes(n):
            quantise(n_codes[:, note_cols[n]], n_scales[:, note_cols[n]], n_grouped[n][:])

        m_grouped = tile("m_grouped", [P, E * PACK], BF16)
        m_codes = tile("m_codes", [P, E], U32)
        m_scales = tile("m_scales", [P, E], U8)

        b_banks, smaller, part, w_tiles, wq_tiles, dl_banks = {}, {}, {}, {}, {}, {}

        def take_smaller(n):
            cols = slice(n * PIECE, (n + 1) * PIECE)
            b_banks[n] = ps.tile([P, PACK, PIECE], F32, name="b_bank", bufs=2)
            for r in range(PACK):
                rows = slice(r * P, (r + 1) * P)
                product(b_banks[n][:, r, :], q2_codes[:, rows].bitcast(FP8X4), q2_scales[:, rows],
                        n_codes[:, cols].bitcast(FP8X4), n_scales[:, cols])
            smaller[n] = tile("smaller%d" % n, [P, PACK, PIECE], F32)
            nc.vector.tensor_tensor(smaller[n][:], b_banks[n][:], a_sb[n][:], ALU.min)

        def add_b(n):
            part[n] = tile("part%d" % n, [P, PACK, PIECE], F32)
            for r in range(PACK):
                nc.vector.scalar_tensor_tensor(
                    part[n][:, r, :], smaller[n][:, r, :], lam_less_one[:, r : r + 1], b_banks[n][:, r, :],
                    ALU.mult, ALU.add,
                )

        def add_a(n):
            s = tile("s_then_dl%d" % n, [P, PIECE * PACK], F32)
            w_tiles[n] = tile("w%d" % n, [P, PIECE * PACK], F32)
            nc.vector.tensor_tensor(
                s[:], part[n][:].rearrange("p r i -> p (r i)"), a_banks[n][:].rearrange("p r i -> p (r i)"), ALU.add
            )
            nc.scalar.activation(
                w_tiles[n][:].rearrange("p (c i r) -> p c r i", i=4, r=PACK),
                s[:].rearrange("p (r c i) -> p c r i", i=4, r=PACK),
                ACT.Sigmoid,
            )

        def weigh(n):
            wq_tiles[n] = tile("wq%d" % n, [P, PIECE * PACK], BF16)
            nc.vector.tensor_tensor(
                wq_tiles[n][:].rearrange("p (i r) -> p i r", r=PACK),
                w_tiles[n][:].rearrange("p (i r) -> p i r", r=PACK),
                qs_cols[:].unsqueeze(1).to_broadcast([P, PIECE, PACK]),
                ALU.mult,
            )

        wq_codes = tile("wq_codes", [P, I], U32)
        wq_scales = tile("wq_scales", [P, I], U8)

        def messages(n, tiles):
            cols = slice(n * PIECE, (n + 1) * PIECE)
            quantise(wq_codes[:, cols], wq_scales[:, cols], wq_tiles[n][:])
            dl_banks[n] = ps.tile([P, PACK, PIECE], F32, name="a_bank%d" % n)
            for place, t in enumerate(tiles):
                rows = slice(t * P, (t + 1) * P)
                product(dl_banks[n][:, place, :], m_codes[:, rows].bitcast(FP8X4), m_scales[:, rows],
                        wq_codes[:, cols].bitcast(FP8X4), wq_scales[:, cols])

        def deliver(n, first, name):
            dl = tile(name, [P, PIECE * 2], F32)
            nc.scalar.copy(dl[:], dl_banks[n][:, first : first + 2, :].rearrange("p t i -> p (t i)"))
            places = place_list[:, n * OFFS_COLS : (n + 1) * OFFS_COLS]
            for k in range(2):
                nc.scalar.activation(windows[first + k][:].indirect(places), dl[:, k * PIECE : (k + 1) * PIECE], ACT.Copy)

        def quantise_msgs(h):
            cols = slice(h * (E // 2), (h + 1) * (E // 2))
            quantise(m_codes[:, cols], m_scales[:, cols], m_grouped[:, h * 2 * E : (h + 1) * 2 * E])

        group_notes(0)
        nc.vector.tensor_copy(q2_view[:, P // 2 : P], q2_halves[1][:].rearrange("p j (m r) -> p m j r", r=PACK))
        quantise_notes(0)
        for r in range(PACK):
            rows = slice(r * P, (r + 1) * P)
            quantise(q2_codes[:, rows], q2_scales[:, rows], q2_grouped[:, r * Q : (r + 1) * Q])
        a_banks = [ps.tile([P, PACK, PIECE], F32, name="a_bank%d" % n) for n in range(PIECES)]
        a_sb = [
            shared.tile([P, PACK, PIECE], F32, name="a_sb%d" % n, offset=off, align_bytes=64)
            for n, off in enumerate((8192, 10240, 12288, 4096))
        ]
        for n in range(PIECES):
            cols = slice(n * PIECE, (n + 1) * PIECE)
            for r in range(PACK):
                rows = slice(r * P, (r + 1) * P)
                product(a_banks[n][:, r, :], q_codes[:, rows].bitcast(FP8X4), q_scales[:, rows],
                        kg_words[:, cols].bitcast(FP4X4), kg_bytes[:, cols])
            nc.scalar.copy(a_sb[n][:], a_banks[n][:])

        group_notes(1)
        group_notes(2)
        for h in range(2):
            cols = slice(h * (E // 2), (h + 1) * (E // 2))
            dst = m_grouped[:, h * 2 * E : (h + 1) * 2 * E].rearrange("p (c i j) -> p c j i", i=4, j=PACK)
            src = msgs_raw[:, :, cols].rearrange("p j (c i) -> p c j i", i=4)
            nc.scalar.copy(dst, src)

        take_smaller(0)
        quantise_notes(1)
        add_b(0)
        add_a(0)
        quantise_msgs(0)
        take_smaller(1)
        weigh(0)
        quantise_msgs(1)
        messages(0, (0, 1, 2, 3))
        add_b(1)
        quantise_notes(2)
        add_a(1)
        deliver(0, 0, "dl0")
        take_smaller(2)
        deliver(0, 2, "s_then_dl1")
        weigh(1)
        add_b(2)
        messages(1, (0, 1))
        add_a(2)
        take_smaller(3)
        deliver(1, 0, "s_then_dl2")
        weigh(2)
        add_b(3)
        messages(2, (0, 1))
        add_a(3)
        deliver(2, 0, "s_then_dl3")
        weigh(3)
        messages(3, (0, 1))
        deliver(3, 0, "dl3")

        def late_product(bank, t, lo, hi):
            rows = slice(t * P, (t + 1) * P)
            product(bank[:, lo:hi], m_codes[:, rows].bitcast(FP8X4), m_scales[:, rows],
                    wq_codes[:, lo:hi].bitcast(FP8X4), wq_scales[:, lo:hi])

        def late_deliver(engine, bank, t, lo, hi):
            late = tile("late%d_%d" % (t, lo), [P, hi - lo], F32)
            target = windows[t][:].indirect(place_list[:, lo // 16 : hi // 16])
            if engine == "vector":
                nc.vector.tensor_copy(late[:], bank[:, lo:hi])
                nc.vector.tensor_copy(target, late[:])
            else:
                nc.scalar.copy(late[:], bank[:, lo:hi])
                nc.scalar.activation(target, late[:], ACT.Copy)

        banks = {}
        for t in (3, 2):
            banks[t] = ps.tile([P, I], F32, name="b_bank", bufs=2)
            late_product(banks[t], t, 2 * PIECE, I)
            late_product(banks[t], t, PIECE, 2 * PIECE)
        late_deliver("vector", banks[3], 3, SPLIT, I)
        late_deliver("scalar", banks[2], 2, PIECE, I)
        late_deliver("scalar", banks[3], 3, PIECE, SPLIT)

        faded = [tile("faded%d" % t, [P, M], F32) for t in range(TILES)]
        for t in order:
            for c in range(FADE_CUTS):
                cols = slice(c * (M // FADE_CUTS), (c + 1) * (M // FADE_CUTS))
                nc.vector.tensor_tensor(faded[t][:, cols], old_tiles[t][:, cols], fade_rows[:, cols], ALU.mult)
        for t in order:
            res = tile("res%d" % t, [P, M], F32)
            edges = (0, M // 2, 3 * M // 4, M) if t == order[-1] else (0, M)
            for lo, hi in zip(edges, edges[1:]):
                nc.vector.tensor_tensor(res[:, lo:hi], faded[t][:, lo:hi], windows[t][:, lo:hi], ALU.add)
                nc.sync.dma_start(out[t * P : (t + 1) * P, lo:hi], res[:, lo:hi])
